import numpy as np
import ml_dtypes


def mxq(x, axis, fmt="e4m3"):
    dtype, down = {"e4m3": (ml_dtypes.float8_e4m3fn, 7), "e5m2": (ml_dtypes.float8_e5m2, 14)}[fmt]
    v = np.moveaxis(np.asarray(x, np.float32).astype(ml_dtypes.bfloat16).astype(np.float64), axis, -1)
    blocks = v.reshape(v.shape[:-1] + (-1, 32))
    amax = np.abs(blocks).max(-1, keepdims=True)
    byte = np.maximum(np.where(amax > 0, np.frexp(amax)[1] - 1 + 127, 0) - down, 1)
    scale = np.exp2(byte - 127.0)
    codes = (blocks / scale).astype(np.float32).astype(dtype).astype(np.float64)
    return np.moveaxis((codes * scale).reshape(v.shape), -1, axis)


WIDE = False


def mx_kscale(k):
    if not WIDE:
        return np.ones(k)
    levels = np.array([10, -10, 5, -5, 0])
    if k % 512:
        return np.exp2(np.random.permutation(np.resize(levels, k // 32))).repeat(32)
    a = np.empty((k // 512, 16))
    for p in range(k // 512):
        a[p, :8] = np.random.permutation(np.resize(levels, 8))
        for g in range(8):
            far = levels[np.abs(levels - a[p, g]) >= 10]
            a[p, g + 8] = far[np.random.randint(len(far))]
    return np.exp2(a.ravel()).repeat(32)


BF16 = ml_dtypes.bfloat16


def bf(x):
    return np.asarray(x, np.float32).astype(BF16)


def f64(x):
    return np.asarray(x).astype(np.float64)


E2M1 = np.array([0.0, 0.5, 1.0, 1.5, 2.0, 3.0, 4.0, 6.0, -0.0, -0.5, -1.0, -1.5, -2.0, -3.0, -4.0, -6.0])


def pack_weight(w, fmt):
    k, n = w.shape
    w = f64(bf(w)).reshape(k // 32, 32, n)
    amax = np.abs(w).max(1)
    if fmt == "e4m3":
        byte = np.frexp(amax)[1] - 1 + 127 - 7
    else:
        mant, ex = np.frexp(amax / 6.0)
        byte = np.where(mant > 0.5, ex, ex - 1) + 127
    byte = np.clip(np.where(amax > 0, byte, 1), 1, 254)
    scaled = (w * np.exp2(127.0 - byte)[:, None, :]).reshape(k, n).astype(np.float32)
    by_word = np.ascontiguousarray(scaled.reshape(k // 512, 128, 4, n).transpose(0, 1, 3, 2))
    if fmt == "e4m3":
        words = by_word.astype(ml_dtypes.float8_e4m3fn).view(np.uint8)
    else:
        c = by_word.astype(ml_dtypes.float4_e2m1fn).view(np.uint8) & 0xF
        words = c[..., 0::2] | (c[..., 1::2] << 4)
    return np.ascontiguousarray(words), np.ascontiguousarray(byte.astype(np.uint8).reshape(k // 512, 16, n))


def unpack_weight(words, scales, fmt):
    g, p, n, _ = words.shape
    if fmt == "e4m3":
        vals = np.ascontiguousarray(words).view(ml_dtypes.float8_e4m3fn).astype(np.float64)
    else:
        nib = np.empty((g, p, n, 4), np.uint8)
        nib[..., 0::2] = words & 0xF
        nib[..., 1::2] = words >> 4
        vals = E2M1[nib]
    vals = vals * np.repeat(np.exp2(scales.astype(np.float64) - 127.0), 8, axis=1)[..., None]
    return vals.transpose(0, 1, 3, 2).reshape(g * 512, n)
def pack4(w):
    words, scales = pack_weight(w, "e2m1")
    return words.reshape(words.shape[0], 128, -1), scales


def unpack4(words, scales):
    return unpack_weight(words.reshape(words.shape[0], 128, -1, 2), scales, "e2m1")


def planes(Y):
    n, m = Y.shape
    b = f64(bf(Y)).reshape(n // 32, 32, m)
    amax = np.abs(b).max(1)
    byte = np.clip(np.where(amax > 0, np.frexp(amax)[1] - 1 + 127 - 7, 1), 1, 254)
    codes = (b * np.exp2(127.0 - byte)[:, None, :]).reshape(n, m).astype(np.float32).astype(ml_dtypes.float8_e4m3fn).view(np.uint8)
    words = codes.reshape(n // 512, 128, 4, m).transpose(0, 1, 3, 2)
    return np.ascontiguousarray(words), np.ascontiguousarray(byte.astype(np.uint8).reshape(n // 512, 16, m))


B, F, D, A, O = 512, 8, 512, 512, 1024


def pair_products(v):
    blocks = []
    for i in range(F - 1):
        blocks.append(v[:, i:i + 1, :] * v[:, i + 1:, :])
    return np.concatenate(blocks, axis=1)


def setup_inputs():
    s, t = mx_kscale(D), mx_kscale(D)
    v = bf(np.random.standard_normal((B, F, D)))
    ga = bf((1.0 + 0.1 * np.random.standard_normal(D)) * s)
    wa_words, wa_scales = pack4(np.random.standard_normal((D, A)) / np.sqrt(D) / s[:, None])
    ba = bf(0.5 * np.random.standard_normal(A))
    h = bf(2.0 * np.random.standard_normal(A) / np.sqrt(A))
    gp = bf((1.0 + 0.1 * np.random.standard_normal(D)) * t)
    wp_words, wp_scales = pack4(3.0 * np.random.standard_normal((D, O)) / np.sqrt(D) / t[:, None])
    return {
        "v": v,
        "ga": ga,
        "wa_words": wa_words,
        "wa_scales": wa_scales,
        "ba": ba,
        "h": h,
        "gp": gp,
        "wp_words": wp_words,
        "wp_scales": wp_scales,
    }


def core(v, ga, wa_words, wa_scales, ba, h, gp, wp_words, wp_scales):
    e = pair_products(f64(v))
    eg = e * f64(ga)[None, None, :]
    z = np.maximum((mxq(eg, 2, "e4m3") @ unpack4(wa_words, wa_scales)) + f64(ba)[None, None, :], 0.0)
    sc = np.sum(z * f64(h)[None, None, :], axis=2)
    p = np.exp(sc - np.max(sc, axis=1, keepdims=True))
    al = p / np.sum(p, axis=1, keepdims=True)
    pool = f64(gp)[None, :] * np.sum(al[:, :, None] * e, axis=1)
    return mxq(pool, 1, "e4m3") @ unpack4(wp_words, wp_scales)


def reference(v, ga, wa_words, wa_scales, ba, h, gp, wp_words, wp_scales):
    R_out = core(v, ga, wa_words, wa_scales, ba, h, gp, wp_words, wp_scales)
    words, scales = planes(R_out.T)
    return R_out, words, scales

@@ -1,0 +1,631 @@
+from contextlib import ExitStack
+
+import concourse.mybir as mybir
+from concourse.masks import make_identity
+
+F32 = mybir.dt.float32
+BF16 = mybir.dt.bfloat16
+U32 = mybir.dt.uint32
+I32 = mybir.dt.int32
+U8 = mybir.dt.uint8
+FP8X4 = mybir.dt.float8_e4m3fn_x4
+FP4X4 = mybir.dt.float4_e2m1fn_x4
+ALU = mybir.AluOpType
+ACTF = mybir.ActivationFunctionType
+AX = mybir.AxisListType
+
+B, F, D, A, O = 512, 8, 512, 512, 1024
+NP = F * (F - 1) // 2
+FLOPS = 2 * B * NP * D * A + 2 * B * D * O
+
+BT = 128
+NT = B // BT
+CPT = NP // 4
+NCH = NT * CPT
+SW = 8
+REP = {0: 1, 2: 1, 1: 1, 3: 1}
+
+
+def pair_of(k):
+    m = 1
+    while m * (m + 1) // 2 <= k:
+        m += 1
+    return m, k - m * (m - 1) // 2
+
+
+PAIRED = (0, 0, 0, 0, 0, 0, 0)
+
+
+def is_paired(c):
+    return True
+
+
+def tile_afmpairattentionpooling_x2_kernel(
+    tc, v, ga, wa_words, wa_scales, ba, h, gp, wp_words, wp_scales, out, out_words, out_scales
+):
+    nc = tc.nc
+    with ExitStack() as ctx:
+        const = ctx.enter_context(tc.tile_pool(name="const", bufs=1))
+        work = ctx.enter_context(tc.tile_pool(name="work", bufs=2))
+        psum = ctx.enter_context(tc.psum_pool(name="psum", bufs=1))
+
+        def keep(shape, dt, name):
+            return const.tile(shape, dt, name=name, tag=name, align_bytes=64)
+
+        def sb(shape, dt, tag, bufs):
+            return work.tile(shape, dt, name=tag, tag=tag, bufs=bufs, align_bytes=64)
+
+        def ps(shape, dt, tag, bufs):
+            return psum.tile(shape, dt, name=tag, tag=tag, bufs=bufs)
+
+        ctx.enter_context(
+            tc.manual_schedule(
+                engines={
+                    mybir.EngineType.PE,
+                    mybir.EngineType.Activation,
+                    mybir.EngineType.DVE,
+                    mybir.EngineType.SP,
+                }
+            )
+        )
+
+        vb = {}
+        vd = {}
+
+        def load_vb(T):
+            for k in range(4):
+                t = sb([128, 2, D], BF16, "vb", 8)
+                nc.sync.dma_start(out=t[:], in_=v[BT * T : BT * (T + 1), 2 * k : 2 * k + 2, :])
+                vb[T, k] = t
+
+        def load_vd(T):
+            t = sb([128, 16, D], BF16, "vd", 2)
+            src = v[BT * T : BT * (T + 1), :, :].rearrange("(g b) j d -> (b j) g d", b=8)
+            for hl in range(2):
+                nc.sync.dma_start(out=t[hl:128:2, :, :], in_=src)
+            vd[T] = t
+
+        ga_b = keep([128, 4], BF16, "ga_b")
+        gp_b = keep([128, 4], BF16, "gp_b")
+        nc.scalar.dma_start(out=ga_b[:], in_=ga.rearrange("(p t) -> p t", t=4))
+        raw = keep([128, 128], BF16, "raw")
+        nc.vector.memset(raw[:], 0.0)
+        wa_sc = keep([128, A], U8, "wa_sc")
+        nc.vector.memset(wa_sc[:].bitcast(I32), 0)
+        wp_sc = keep([128, O], U8, "wp_sc")
+        nc.vector.memset(wp_sc[:].bitcast(I32), 0)
+        nc.scalar.dma_start(out=raw[0:4, :], in_=h.rearrange("(r c) -> r c", c=128))
+        nc.scalar.dma_start(out=raw[4:8, :], in_=ba.rearrange("(r c) -> r c", c=128))
+        for q in range(4):
+            nc.scalar.dma_start(
+                out=wa_sc[32 * q : 32 * q + 4, :].bitcast(I32),
+                in_=wa_scales[0, 4 * q : 4 * q + 4, :].bitcast(I32),
+            )
+        load_vb(0)
+        wa_sb = keep([128, 2 * A], U8, "wa_sb")
+        nc.sync.dma_start(out=wa_sb[:], in_=wa_words[0, :, :])
+        wp_sb = keep([128, 2 * O], U8, "wp_sb")
+        nc.sync.dma_start(out=wp_sb[:], in_=wp_words[0, :, :])
+        for q in range(4):
+            nc.sync.dma_start(
+                out=wp_sc[32 * q : 32 * q + 4, :].bitcast(I32),
+                in_=wp_scales[0, 4 * q : 4 * q + 4, :].bitcast(I32),
+            )
+        nc.sync.dma_start(out=gp_b[:], in_=gp.rearrange("(p t) -> p t", t=4))
+        load_vb(1)
+        load_vd(0)
+
+        ident = keep([128, 128], F32, "ident")
+        make_identity(nc, ident[:])
+        ident_b = keep([128, 128], BF16, "ident_b")
+        nc.vector.tensor_copy(out=ident_b[:], in_=ident[:])
+        ga_f = keep([128, 4], F32, "ga_f")
+        nc.vector.tensor_copy(out=ga_f[:], in_=ga_b[:])
+
+        rawT = ps([128, 128], BF16, "m", 3)
+        nc.tensor.transpose(rawT[:], raw[:], ident_b[:])
+        hb = keep([128, 8], F32, "hb")
+        nc.vector.tensor_copy(out=hb[:], in_=rawT[:, 0:8])
+        hc = hb[:, 0:4]
+        bac = hb[:, 4:8]
+        nba = keep([128, 4], F32, "nba")
+        nc.vector.tensor_scalar(out=nba[:], in0=bac, scalar1=-1.0, scalar2=None, op0=ALU.mult)
+        hsq = keep([128, 2], F32, "hsq")
+        nc.vector.tensor_tensor(out=hsq[:], in0=hb[:, 1:4:2], in1=hb[:, 1:4:2], op=ALU.mult)
+        hmask = keep([128, 2], F32, "hmask")
+        nc.vector.tensor_scalar(
+            out=hmask[:], in0=hsq[:], scalar1=1e-36, scalar2=4e-18, op0=ALU.is_lt, op1=ALU.mult
+        )
+        hodd = keep([128, 2], F32, "hodd")
+        nc.vector.tensor_tensor(out=hodd[:], in0=hb[:, 1:4:2], in1=hmask[:], op=ALU.add)
+        hrec = keep([128, 2], F32, "hrec")
+        nc.vector.reciprocal(out=hrec[:], in_=hodd[:])
+        ratio = keep([128, 2], F32, "ratio")
+        nc.vector.tensor_tensor(out=ratio[:], in0=hb[:, 0:4:2], in1=hrec[:], op=ALU.mult)
+
+        wide = keep([128, 6, SW], F32, "wide")
+        nc.vector.tensor_copy(
+            out=wide[:, 0:4, :], in_=hb[:, 0:4].unsqueeze(2).to_broadcast([128, 4, SW])
+        )
+        nc.vector.tensor_copy(
+            out=wide[:, 4:6, :], in_=hodd[:].unsqueeze(2).to_broadcast([128, 2, SW])
+        )
+
+        vT = {}
+        vg = {}
+        trb = {}
+
+        def prep_tr(T, k):
+            if k == 0:
+                vT[T] = sb([128, F, BT, 4], BF16, "vT", 3)
+                vg[T] = sb([128, F - 1, 4, BT], F32, "vg", 2)
+            bank = ps([128, 2, 2, 128], F32, "m", 3)
+            words = vb[T, k][:].rearrange("p f d -> p (f d)").bitcast(F32)
+            for f in range(2):
+                for u in range(2):
+                    nc.tensor.transpose(
+                        bank[:, f, u, :], words[:, 256 * f + u : 256 * (f + 1) : 2], ident[:]
+                    )
+            trb[T, k] = bank
+
+        def prep_act(T, k):
+            bank = trb.pop((T, k))
+            nc.scalar.copy(
+                out=vT[T][:].bitcast(F32)[:, 2 * k : 2 * k + 2, :, :],
+                in_=bank[:].rearrange("p f u b -> p f b u"),
+            )
+            half = bank[:].bitcast(BF16).rearrange("p f u (b e) -> p f u b e", e=2)
+            f0 = 1 if k == 0 else 0
+            for t in range(4):
+                nc.scalar.activation(
+                    out=vg[T][:, 2 * k + f0 - 1 : 2 * k + 1, t, :],
+                    in_=half[:, f0:2, t // 2, :, t % 2],
+                    func=ACTF.Copy,
+                    scale=ga_f[:, t : t + 1],
+                )
+
+        for k in range(4):
+            prep_tr(0, k)
+            prep_act(0, k)
+
+        wsel = keep([128, F - 1, 240], BF16, "wsel")
+        nc.gpsimd.memset(wsel[:], 0.0)
+        for m in range(1, F):
+            r0 = m * (m - 1)
+            nc.gpsimd.tensor_copy(
+                out=wsel[:, m - 1, 112 : 112 + 2 * m], in_=ident_b[:, r0 : r0 + 2 * m]
+            )
+        comps = []
+        for i in range(2):
+            cp = keep([128, 64, 2], BF16, "comp%d" % i)
+            nc.gpsimd.memset(cp[:], 0.0)
+            comps.append(cp)
+        bmask = keep([128, 8], BF16, "bmask")
+        bmask_f = keep([128, 8], F32, "bmask_f")
+        nc.vector.tensor_reduce(
+            out=bmask_f[:], in_=ident[:].rearrange("p (b r) -> p b r", r=16), axis=AX.X, op=ALU.add
+        )
+        nc.vector.tensor_copy(out=bmask[:], in_=bmask_f[:])
+        gp_f = keep([128, 4], F32, "gp_f")
+        nc.gpsimd.tensor_copy(out=gp_f[:], in_=gp_b[:])
+        wpp = keep([128, 2 * O], U8, "wpp")
+        wpp_sc = keep([128, O], U8, "wpp_sc")
+        for g in range(2):
+            nc.gpsimd.tensor_copy(
+                out=wpp[:, 1024 * g : 1024 * (g + 1)].rearrange("p (t m c) -> p t m c", t=4, c=2),
+                in_=wp_sb[:, 1024 * g : 1024 * (g + 1)].rearrange("p (m t c) -> p t m c", t=4, c=2),
+            )
+            nc.gpsimd.tensor_copy(
+                out=wpp_sc[:, 512 * g : 512 * (g + 1)].rearrange("p (t m) -> p t m", t=4),
+                in_=wp_sc[:, 512 * g : 512 * (g + 1)].rearrange("p (m t) -> p t m", t=4),
+            )
+
+        egs = {}
+        cod = {}
+        zb = {}
+        ys = {}
+        S = {}
+
+        def eg_step(c):
+            T, cc = divmod(c, CPT)
+            eg = sb([128, 4, BT, 4], BF16, "eg", 3)
+            s = 0
+            while s < 4:
+                m, j = pair_of(4 * cc + s)
+                n = min(4 - s, m - j)
+                nc.vector.tensor_tensor(
+                    out=eg[:, s : s + n, :, :],
+                    in0=vg[T][:, m - 1, :, :]
+                    .rearrange("p t b -> p b t")
+                    .unsqueeze(1)
+                    .to_broadcast([128, n, BT, 4]),
+                    in1=vT[T][:, j : j + n, :, :],
+                    op=ALU.mult,
+                )
+                s += n
+            egs[c] = eg
+
+        def q_step(c):
+            eg = egs.pop(c)
+            codes = sb([128, 512], U32, "codes", 3)
+            scales = sb([128, 512], U8, "scales", 3)
+            nc.vector.quantize_mx(
+                out=codes[:].bitcast(FP8X4),
+                scales=scales[:],
+                in_=eg[:].rearrange("p s b t -> p (s b t)"),
+            )
+            cod[c] = (codes, scales)
+
+        def mx_step(c, a):
+            codes, scales = cod[c]
+            z = ps([128, 512], F32, "z", 4)
+            for rep in range(REP[a]):
+                nc.tensor.matmul_mx(
+                    out=z[:],
+                    lhsT=wa_sb[:, 256 * a : 256 * (a + 1)].bitcast(FP4X4),
+                    lhsT_scale=wa_sc[:, 128 * a : 128 * (a + 1)],
+                    rhs=codes[:].bitcast(FP8X4),
+                    rhs_scale=scales[:],
+                    start=True,
+                    stop=True,
+                )
+            zb.setdefault(c, {})[a] = z
+
+        def relu_out(z, a):
+            y = sb([128, 512], F32, "y", 11)
+            nc.scalar.activation(
+                out=y[:], in_=z[:], func=ACTF.Relu, bias=bac[:, a : a + 1], scale=1.0
+            )
+            return y
+
+        def evac_step(c):
+            zz = zb[c]
+            if is_paired(c):
+                parts = []
+                for i in range(2):
+                    y = relu_out(zz[2 * i], 2 * i)
+                    yc = sb([128, 512], F32, "yc", 5)
+                    nc.scalar.activation(
+                        out=yc[:],
+                        in_=y[:],
+                        func=ACTF.Identity,
+                        scale=ratio[:, i : i + 1],
+                        bias=bac[:, 2 * i + 1 : 2 * i + 2],
+                    )
+                    parts.append(yc)
+                ys[c] = parts
+            else:
+                ys[c] = [(relu_out(zz[a], a), wide[:, a, :]) for a in range(4)]
+
+        def stt_step(c):
+            if not is_paired(c):
+                return
+            parts = []
+            for i in range(2):
+                r = sb([128, 512], F32, "r", 5)
+                nc.vector.scalar_tensor_tensor(
+                    out=r[:],
+                    in0=zb[c][2 * i + 1][:],
+                    scalar=nba[:, 2 * i + 1 : 2 * i + 2],
+                    in1=ys[c][i][:],
+                    op0=ALU.max,
+                    op1=ALU.add,
+                )
+                parts.append((r, wide[:, 4 + i, :]))
+            ys[c] = parts
+
+        def score_step(c, s):
+            T, cc = divmod(c, CPT)
+            if cc == 0 and s == 0:
+                S[T] = ps([128, NP, SW], F32, "s", 1)
+            parts = ys[c]
+            col = 4 * cc + s
+            for i, (y, w) in enumerate(parts):
+                nc.tensor.matmul(
+                    S[T][:, col, :],
+                    lhsT=y[:, 128 * s : 128 * (s + 1)],
+                    rhs=w,
+                    start=(i == 0),
+                    stop=(i == len(parts) - 1),
+                )
+
+        st = {}
+
+        def soft_a(T):
+            ssb = sb([128, NP], F32, "ssb", 2)
+            nc.vector.tensor_copy(out=ssb[:], in_=S.pop(T)[:, :, 0])
+            mx = sb([128, 1], F32, "mx", 2)
+            nc.vector.tensor_reduce(out=mx[:], in_=ssb[:], axis=AX.X, op=ALU.max)
+            nmx = sb([128, 1], F32, "nmx", 2)
+            nc.vector.tensor_scalar(
+                out=nmx[:], in0=mx[:], scalar1=-1.0, scalar2=None, op0=ALU.mult
+            )
+            st["soft", T] = (ssb, nmx)
+
+        def soft_exp(T):
+            ssb, nmx = st.pop(("soft", T))
+            e = sb([128, NP], F32, "e", 2)
+            zs = sb([128, 1], F32, "zs", 2)
+            nc.scalar.activation(
+                out=e[:], in_=ssb[:], func=ACTF.Exp, bias=nmx[:], scale=1.0, accum_out=zs[:]
+            )
+            st["exp", T] = (e, zs)
+
+        def soft_b(T):
+            e, zs = st.pop(("exp", T))
+            rz = sb([128, 1], F32, "rz", 2)
+            nc.vector.reciprocal(out=rz[:], in_=zs[:])
+            al = sb([128, NP], F32, "al", 2)
+            nc.vector.tensor_scalar(
+                out=al[:], in0=e[:], scalar1=rz[:], scalar2=None, op0=ALU.mult
+            )
+            cp = comps[T % 2]
+            nc.vector.tensor_copy(out=cp[:, 0:NP, 0], in_=al[:])
+            nc.vector.tensor_tensor(
+                out=cp[:, 0:NP, 1], in0=al[:], in1=cp[:, 0:NP, 0], op=ALU.subtract
+            )
+
+        def al_tr(T):
+            bank = ps([128, 128], BF16, "m", 3)
+            nc.tensor.transpose(
+                bank[:], comps[T % 2][:].rearrange("p k c -> p (k c)"), ident_b[:]
+            )
+            st["alb", T] = bank
+
+        def al_copy(T):
+            bank = st.pop(("alb", T))
+            alT = sb([128, 128], BF16, "alT", 2)
+            nc.scalar.copy(out=alT[:], in_=bank[:])
+            st["alT", T] = alT
+
+        def sel(T):
+            alT = st.pop(("alT", T))
+            bank = ps([128, F - 1, 16], F32, "m", 3)
+            rhs = alT[:].rearrange("p (g b) -> p b g", b=8)
+            for m in range(F - 1):
+                for b in range(8):
+                    nc.tensor.matmul(
+                        bank[:, m, :],
+                        lhsT=wsel[:, m, 112 - 16 * b : 240 - 16 * b],
+                        rhs=rhs[:, b, :],
+                        start=(b == 0),
+                        stop=(b == 7),
+                    )
+            st["sel", T] = bank
+
+        def make_ap(T):
+            bank = st.pop(("sel", T))
+            ap = sb([128, 16, F - 1, 8], BF16, "ap", 2)
+            nc.vector.tensor_tensor(
+                out=ap[:],
+                in0=bank[:].rearrange("p m g -> p g m").unsqueeze(3).to_broadcast([128, 16, F - 1, 8]),
+                in1=bmask[:].unsqueeze(1).unsqueeze(1).to_broadcast([128, 16, F - 1, 8]),
+                op=ALU.mult,
+            )
+            st["ap", T] = ap
+
+        def pool_mm(T, dg):
+            ap = st["ap", T]
+            bank = ps([128, 4, F - 1, 16], F32, "m", 3)
+            for gi in range(2):
+                g = 2 * dg + gi
+                for t in range(4):
+                    nc.tensor.matmul(
+                        bank[:, t, :, 8 * gi : 8 * gi + 8],
+                        lhsT=vd[T][:, g, t : D : 4],
+                        rhs=ap[:, g, :, :],
+                        start=True,
+                        stop=True,
+                    )
+            st["pm", T, dg] = bank
+
+        def pool_mul(T, dg):
+            bank = st.pop(("pm", T, dg))
+            if dg == 0:
+                st["q", T] = sb([128, 4, F - 1, BT], F32, "q", 2)
+            q = st["q", T]
+            nc.vector.tensor_tensor(
+                out=q[:, :, :, 16 * dg : 16 * dg + 16],
+                in0=bank[:],
+                in1=vT[T][:, 1:F, 16 * dg : 16 * dg + 16, :].rearrange("p m b t -> p t m b"),
+                op=ALU.mult,
+            )
+
+        def pool_sum(T):
+            q = st.pop(("q", T))
+            bank = ps([128, 4, 128], F32, "m", 3)
+            for t in range(4):
+                for m in range(F - 1):
+                    nc.tensor.matmul(
+                        bank[:, t, :],
+                        lhsT=q[:, t, m, :],
+                        rhs=ident[:],
+                        start=(m == 0),
+                        stop=(m == F - 2),
+                        is_transpose=True,
+                    )
+            st["sum", T] = bank
+
+        def sum_copy(T):
+            bank = st.pop(("sum", T))
+            psb = sb([128, 4, 128], F32, "psb", 2)
+            nc.scalar.copy(out=psb[:], in_=bank[:])
+            st["psb", T] = psb
+
+        def pool_back(T):
+            psb = st.pop(("psb", T))
+            bank = ps([128, 4, BT], F32, "m", 3)
+            for t in range(4):
+                nc.tensor.transpose(bank[:, t, :], psb[:, t, :], ident[:])
+            st["back", T] = bank
+
+        def pool_gain(T):
+            bank = st.pop(("back", T))
+            pl = sb([128, BT, 4], BF16, "pl", 2)
+            nc.vector.tensor_tensor(
+                out=pl[:],
+                in0=bank[:].rearrange("p t b -> p b t"),
+                in1=gp_f[:].unsqueeze(1).to_broadcast([128, BT, 4]),
+                op=ALU.mult,
+            )
+            st["pl", T] = pl
+
+        osc = keep([128, 2, B], U8, "osc")
+
+        def head_q(T):
+            pl = st.pop(("pl", T))
+            pc = sb([128, BT], U32, "pc", 2)
+            psc = sb([128, BT], U8, "psc", 2)
+            nc.vector.quantize_mx(
+                out=pc[:].bitcast(FP8X4), scales=psc[:], in_=pl[:].rearrange("p b t -> p (b t)")
+            )
+            st["pc", T] = (pc, psc)
+
+        def head_p(T, g):
+            pc, psc = st["pc", T]
+            bank = ps([128, 4, BT], F32, "m", 3)
+            for t in range(4):
+                col = 512 * g + 128 * t
+                nc.tensor.matmul_mx(
+                    out=bank[:, t, :],
+                    lhsT=wpp[:, 2 * col : 2 * col + 256].bitcast(FP4X4),
+                    lhsT_scale=wpp_sc[:, col : col + 128],
+                    rhs=pc[:].bitcast(FP8X4),
+                    rhs_scale=psc[:],
+                    start=True,
+                    stop=True,
+                )
+            st["pbank", T, g] = bank
+
+        def head_pe(T, g):
+            bank = st.pop(("pbank", T, g))
+            pb = sb([128, BT, 4], BF16, "pb", 4)
+            nc.scalar.copy(out=pb[:], in_=bank[:].rearrange("p t b -> p b t"))
+            st["pb", T, g] = pb
+
+        def head_pq(T, g):
+            pb = st.pop(("pb", T, g))
+            oc = sb([128, BT], U32, "oc", 4)
+            nc.vector.quantize_mx(
+                out=oc[:].bitcast(FP8X4),
+                scales=osc[:, g, BT * T : BT * (T + 1)],
+                in_=pb[:].rearrange("p b t -> p (b t)"),
+            )
+            nc.sync.dma_start(
+                out=out_words[g, :, BT * T : BT * (T + 1), :]
+                .rearrange("p m t -> p (m t)")
+                .bitcast(I32),
+                in_=oc[:].bitcast(I32),
+            )
+            if T == NT - 1:
+                for q in range(4):
+                    eng = nc.sync if q % 2 else nc.scalar
+                    eng.dma_start(
+                        out=out_scales[g, 4 * q : 4 * q + 4, :].bitcast(I32),
+                        in_=osc[32 * q : 32 * q + 4, g, :].bitcast(I32),
+                    )
+
+        def head_o(T, hf):
+            pc, psc = st["pc", T]
+            bank = ps([128, 512], F32, "m", 3)
+            nc.tensor.matmul_mx(
+                out=bank[:],
+                lhsT=pc[:].bitcast(FP8X4),
+                lhsT_scale=psc[:],
+                rhs=wp_sb[:, 1024 * hf : 1024 * (hf + 1)].bitcast(FP4X4),
+                rhs_scale=wp_sc[:, 512 * hf : 512 * (hf + 1)],
+                start=True,
+                stop=True,
+            )
+            st["obank", T, hf] = bank
+
+        def head_oe(T, hf):
+            bank = st.pop(("obank", T, hf))
+            o = sb([128, 512], F32, "o", 4)
+            nc.scalar.copy(out=o[:], in_=bank[:])
+            nc.sync.dma_start(
+                out=out[BT * T : BT * (T + 1), 512 * hf : 512 * (hf + 1)], in_=o[:]
+            )
+
+        pre = {
+            3: [(al_copy,)],
+            4: [(make_ap,)],
+            5: [(pool_mul, 0), (pool_mul, 1)],
+            6: [(pool_mul, 2), (pool_mul, 3)],
+            7: [(pool_mul, 4), (pool_mul, 5)],
+            8: [(pool_mul, 6), (pool_mul, 7)],
+            9: [(sum_copy,)],
+            10: [(pool_gain,)],
+            11: [(head_pe, 0), (head_oe, 0)],
+            12: [(head_pe, 1), (head_pq, 0)],
+            13: [(head_oe, 1), (head_pq, 1)],
+        }
+        mid = {2: [(soft_b,)], 10: [(head_q,)]}
+        pes = {
+            2: [(al_tr,)],
+            3: [(sel,)],
+            4: [(pool_mm, 0), (pool_mm, 1)],
+            5: [(pool_mm, 2), (pool_mm, 3)],
+            6: [(pool_mm, 4), (pool_mm, 5)],
+            7: [(pool_mm, 6), (pool_mm, 7)],
+            8: [(pool_sum,)],
+            9: [(pool_back,)],
+            10: [(head_p, 0), (head_o, 0)],
+            11: [(head_p, 1)],
+            12: [(head_o, 1)],
+        }
+        prep_at = {}
+        for T in range(1, NT):
+            for q, k in ((0, 0), (2, 1), (3, 2), (5, 3)):
+                prep_at.setdefault(CPT * (T - 1) + q + (1 if T == 1 and q < 1 else 0), []).append((T, k))
+        late = []
+        eg_step(0)
+
+        for n in range(NCH + 14):
+            offs = [(T, n - CPT * (T + 1)) for T in range(NT) if 0 <= n - CPT * (T + 1) <= 13]
+            offs.reverse()
+
+            def run(table):
+                for T, o in offs:
+                    for f, *args in table.get(o, []):
+                        f(T, *args)
+
+            for T, o in offs:
+                if o == 2:
+                    soft_a(T)
+            if n < NCH:
+                q_step(n)
+                mx_step(n, 0)
+                mx_step(n, 2)
+            if 2 <= n <= NCH + 1:
+                score_step(n - 2, 0)
+                score_step(n - 2, 1)
+            if 1 <= n <= NCH:
+                stt_step(n - 1)
+            if n < NCH:
+                mx_step(n, 1)
+            if 2 <= n <= NCH + 1:
+                score_step(n - 2, 2)
+                score_step(n - 2, 3)
+            if n < NCH:
+                mx_step(n, 3)
+            for T, o in offs:
+                if o == 2:
+                    soft_exp(T)
+            run(pre)
+            if n < NCH:
+                evac_step(n)
+            for T, k in late:
+                prep_act(T, k)
+            late = []
+            if n + 1 < NCH:
+                eg_step(n + 1)
+            run(mid)
+            run(pes)
+            for T, k in prep_at.get(n, []):
+                prep_tr(T, k)
+                late.append((T, k))
+            if n % CPT == 0 and n // CPT + 2 < NT:
+                load_vb(n // CPT + 2)
+            if n % CPT == 0 and 0 < n // CPT < NT:
+                load_vd(n // CPT)

@@ -33,11 +33,7 @@ def pair_of(k):
     return m, k - m * (m - 1) // 2
 
 
-PAIRED = (0, 0, 0, 0, 0, 0, 0)
-
-
-def is_paired(c):
-    return True
+MODES = [1] * 28
 
 
 def tile_afmpairattentionpooling_x2_kernel(
@@ -143,6 +139,8 @@ def tile_afmpairattentionpooling_x2_kernel(
         ratio = keep([128, 2], F32, "ratio")
         nc.vector.tensor_tensor(out=ratio[:], in0=hb[:, 0:4:2], in1=hrec[:], op=ALU.mult)
 
+        ratio2 = keep([128, 1], F32, "ratio2")
+        nc.vector.tensor_tensor(out=ratio2[:], in0=hodd[:, 0:1], in1=hrec[:, 1:2], op=ALU.mult)
         wide = keep([128, 6, SW], F32, "wide")
         nc.vector.tensor_copy(
             out=wide[:, 0:4, :], in_=hb[:, 0:4].unsqueeze(2).to_broadcast([128, 4, SW])
@@ -232,14 +230,11 @@ def tile_afmpairattentionpooling_x2_kernel(
             s = 0
             while s < 4:
                 m, j = pair_of(4 * cc + s)
-                n = min(4 - s, m - j)
+                n = 1
                 nc.vector.tensor_tensor(
-                    out=eg[:, s : s + n, :, :],
-                    in0=vg[T][:, m - 1, :, :]
-                    .rearrange("p t b -> p b t")
-                    .unsqueeze(1)
-                    .to_broadcast([128, n, BT, 4]),
-                    in1=vT[T][:, j : j + n, :, :],
+                    out=eg[:, s, :, :].rearrange("p (c i) t -> p c t i", i=4),
+                    in0=vg[T][:, m - 1, :, :].rearrange("p t (c i) -> p c t i", i=4),
+                    in1=vT[T][:, j, :, :].rearrange("p (c i) t -> p c t i", i=4),
                     op=ALU.mult,
                 )
                 s += n
@@ -280,7 +275,7 @@ def tile_afmpairattentionpooling_x2_kernel(
 
         def evac_step(c):
             zz = zb[c]
-            if is_paired(c):
+            if MODES[c]:
                 parts = []
                 for i in range(2):
                     y = relu_out(zz[2 * i], 2 * i)
@@ -298,7 +293,7 @@ def tile_afmpairattentionpooling_x2_kernel(
                 ys[c] = [(relu_out(zz[a], a), wide[:, a, :]) for a in range(4)]
 
         def stt_step(c):
-            if not is_paired(c):
+            if not MODES[c]:
                 return
             parts = []
             for i in range(2):
@@ -313,6 +308,16 @@ def tile_afmpairattentionpooling_x2_kernel(
                 )
                 parts.append((r, wide[:, 4 + i, :]))
             ys[c] = parts
+
+        def comb_step(c):
+            if MODES[c] != 2:
+                return
+            (r0, w0), (r1, w1) = ys[c]
+            r = sb([128, 512], F32, "rr", 3)
+            nc.vector.scalar_tensor_tensor(
+                out=r[:], in0=r0[:], scalar=ratio2[:], in1=r1[:], op0=ALU.mult, op1=ALU.add
+            )
+            ys[c] = [(r, w1)]
 
         def score_step(c, s):
             T, cc = divmod(c, CPT)
@@ -406,7 +411,7 @@ def tile_afmpairattentionpooling_x2_kernel(
 
         def pool_mm(T, dg):
             ap = st["ap", T]
-            bank = ps([128, 4, F - 1, 16], F32, "m", 3)
+            bank = ps([128, 4, F - 1, 16], F32, *(("z", 4) if T == NT - 1 else ("m", 3)))
             for gi in range(2):
                 g = 2 * dg + gi
                 for t in range(4):
@@ -620,6 +625,8 @@ def tile_afmpairattentionpooling_x2_kernel(
             late = []
             if n + 1 < NCH:
                 eg_step(n + 1)
+            if 1 <= n <= NCH:
+                comb_step(n - 1)
             run(mid)
             run(pes)
             for T, k in prep_at.get(n, []):

from contextlib import ExitStack

import concourse.mybir as mybir
from concourse.masks import make_identity

F32 = mybir.dt.float32
BF16 = mybir.dt.bfloat16
U32 = mybir.dt.uint32
I32 = mybir.dt.int32
U8 = mybir.dt.uint8
FP8X4 = mybir.dt.float8_e4m3fn_x4
FP4X4 = mybir.dt.float4_e2m1fn_x4
ALU = mybir.AluOpType
ACTF = mybir.ActivationFunctionType
AX = mybir.AxisListType

B, F, D, A, O = 512, 8, 512, 512, 1024
NP = F * (F - 1) // 2
FLOPS = 2 * B * NP * D * A + 2 * B * D * O

BT = 128
NT = B // BT
CPT = NP // 4
NCH = NT * CPT
SW = 8
REP = {0: 1, 2: 1, 1: 1, 3: 1}


def pair_of(k):
    m = 1
    while m * (m + 1) // 2 <= k:
        m += 1
    return m, k - m * (m - 1) // 2


MODES = [1] * 28


def tile_afmpairattentionpooling_x2_kernel(
    tc, v, ga, wa_words, wa_scales, ba, h, gp, wp_words, wp_scales, out, out_words, out_scales
):
    nc = tc.nc
    with ExitStack() as ctx:
        const = ctx.enter_context(tc.tile_pool(name="const", bufs=1))
        work = ctx.enter_context(tc.tile_pool(name="work", bufs=2))
        psum = ctx.enter_context(tc.psum_pool(name="psum", bufs=1))

        def keep(shape, dt, name):
            return const.tile(shape, dt, name=name, tag=name, align_bytes=64)

        def sb(shape, dt, tag, bufs):
            return work.tile(shape, dt, name=tag, tag=tag, bufs=bufs, align_bytes=64)

        def ps(shape, dt, tag, bufs):
            return psum.tile(shape, dt, name=tag, tag=tag, bufs=bufs)

        ctx.enter_context(
            tc.manual_schedule(
                engines={
                    mybir.EngineType.PE,
                    mybir.EngineType.Activation,
                    mybir.EngineType.DVE,
                    mybir.EngineType.SP,
                }
            )
        )

        vb = {}
        vd = {}

        def load_vb(T):
            for k in range(4):
                t = sb([128, 2, D], BF16, "vb", 8)
                nc.sync.dma_start(out=t[:], in_=v[BT * T : BT * (T + 1), 2 * k : 2 * k + 2, :])
                vb[T, k] = t

        def load_vd(T):
            t = sb([128, 16, D], BF16, "vd", 2)
            src = v[BT * T : BT * (T + 1), :, :].rearrange("(g b) j d -> (b j) g d", b=8)
            for hl in range(2):
                nc.sync.dma_start(out=t[hl:128:2, :, :], in_=src)
            vd[T] = t

        ga_b = keep([128, 4], BF16, "ga_b")
        gp_b = keep([128, 4], BF16, "gp_b")
        nc.scalar.dma_start(out=ga_b[:], in_=ga.rearrange("(p t) -> p t", t=4))
        raw = keep([128, 128], BF16, "raw")
        nc.vector.memset(raw[:], 0.0)
        wa_sc = keep([128, A], U8, "wa_sc")
        nc.vector.memset(wa_sc[:].bitcast(I32), 0)
        wp_sc = keep([128, O], U8, "wp_sc")
        nc.vector.memset(wp_sc[:].bitcast(I32), 0)
        nc.scalar.dma_start(out=raw[0:4, :], in_=h.rearrange("(r c) -> r c", c=128))
        nc.scalar.dma_start(out=raw[4:8, :], in_=ba.rearrange("(r c) -> r c", c=128))
        for q in range(4):
            nc.scalar.dma_start(
                out=wa_sc[32 * q : 32 * q + 4, :].bitcast(I32),
                in_=wa_scales[0, 4 * q : 4 * q + 4, :].bitcast(I32),
            )
        load_vb(0)
        wa_sb = keep([128, 2 * A], U8, "wa_sb")
        nc.sync.dma_start(out=wa_sb[:], in_=wa_words[0, :, :])
        wp_sb = keep([128, 2 * O], U8, "wp_sb")
        nc.sync.dma_start(out=wp_sb[:], in_=wp_words[0, :, :])
        for q in range(4):
            nc.sync.dma_start(
                out=wp_sc[32 * q : 32 * q + 4, :].bitcast(I32),
                in_=wp_scales[0, 4 * q : 4 * q + 4, :].bitcast(I32),
            )
        nc.sync.dma_start(out=gp_b[:], in_=gp.rearrange("(p t) -> p t", t=4))
        load_vb(1)
        load_vd(0)

        ident = keep([128, 128], F32, "ident")
        make_identity(nc, ident[:])
        ident_b = keep([128, 128], BF16, "ident_b")
        nc.vector.tensor_copy(out=ident_b[:], in_=ident[:])
        ga_f = keep([128, 4], F32, "ga_f")
        nc.vector.tensor_copy(out=ga_f[:], in_=ga_b[:])

        rawT = ps([128, 128], BF16, "m", 3)
        nc.tensor.transpose(rawT[:], raw[:], ident_b[:])
        hb = keep([128, 8], F32, "hb")
        nc.vector.tensor_copy(out=hb[:], in_=rawT[:, 0:8])
        hc = hb[:, 0:4]
        bac = hb[:, 4:8]
        nba = keep([128, 4], F32, "nba")
        nc.vector.tensor_scalar(out=nba[:], in0=bac, scalar1=-1.0, scalar2=None, op0=ALU.mult)
        hsq = keep([128, 2], F32, "hsq")
        nc.vector.tensor_tensor(out=hsq[:], in0=hb[:, 1:4:2], in1=hb[:, 1:4:2], op=ALU.mult)
        hmask = keep([128, 2], F32, "hmask")
        nc.vector.tensor_scalar(
            out=hmask[:], in0=hsq[:], scalar1=1e-36, scalar2=4e-18, op0=ALU.is_lt, op1=ALU.mult
        )
        hodd = keep([128, 2], F32, "hodd")
        nc.vector.tensor_tensor(out=hodd[:], in0=hb[:, 1:4:2], in1=hmask[:], op=ALU.add)
        hrec = keep([128, 2], F32, "hrec")
        nc.vector.reciprocal(out=hrec[:], in_=hodd[:])
        ratio = keep([128, 2], F32, "ratio")
        nc.vector.tensor_tensor(out=ratio[:], in0=hb[:, 0:4:2], in1=hrec[:], op=ALU.mult)

        ratio2 = keep([128, 1], F32, "ratio2")
        nc.vector.tensor_tensor(out=ratio2[:], in0=hodd[:, 0:1], in1=hrec[:, 1:2], op=ALU.mult)
        wide = keep([128, 6, SW], F32, "wide")
        nc.vector.tensor_copy(
            out=wide[:, 0:4, :], in_=hb[:, 0:4].unsqueeze(2).to_broadcast([128, 4, SW])
        )
        nc.vector.tensor_copy(
            out=wide[:, 4:6, :], in_=hodd[:].unsqueeze(2).to_broadcast([128, 2, SW])
        )

        vT = {}
        vg = {}
        trb = {}

        def prep_tr(T, k):
            if k == 0:
                vT[T] = sb([128, F, BT, 4], BF16, "vT", 3)
                vg[T] = sb([128, F - 1, 4, BT], F32, "vg", 2)
            bank = ps([128, 2, 2, 128], F32, "m", 3)
            words = vb[T, k][:].rearrange("p f d -> p (f d)").bitcast(F32)
            for f in range(2):
                for u in range(2):
                    nc.tensor.transpose(
                        bank[:, f, u, :], words[:, 256 * f + u : 256 * (f + 1) : 2], ident[:]
                    )
            trb[T, k] = bank

        def prep_act(T, k):
            bank = trb.pop((T, k))
            nc.scalar.copy(
                out=vT[T][:].bitcast(F32)[:, 2 * k : 2 * k + 2, :, :],
                in_=bank[:].rearrange("p f u b -> p f b u"),
            )
            half = bank[:].bitcast(BF16).rearrange("p f u (b e) -> p f u b e", e=2)
            f0 = 1 if k == 0 else 0
            for t in range(4):
                nc.scalar.activation(
                    out=vg[T][:, 2 * k + f0 - 1 : 2 * k + 1, t, :],
                    in_=half[:, f0:2, t // 2, :, t % 2],
                    func=ACTF.Copy,
                    scale=ga_f[:, t : t + 1],
                )

        for k in range(4):
            prep_tr(0, k)
            prep_act(0, k)

        wsel = keep([128, F - 1, 240], BF16, "wsel")
        nc.gpsimd.memset(wsel[:], 0.0)
        for m in range(1, F):
            r0 = m * (m - 1)
            nc.gpsimd.tensor_copy(
                out=wsel[:, m - 1, 112 : 112 + 2 * m], in_=ident_b[:, r0 : r0 + 2 * m]
            )
        comps = []
        for i in range(2):
            cp = keep([128, 64, 2], BF16, "comp%d" % i)
            nc.gpsimd.memset(cp[:], 0.0)
            comps.append(cp)
        bmask = keep([128, 8], BF16, "bmask")
        bmask_f = keep([128, 8], F32, "bmask_f")
        nc.vector.tensor_reduce(
            out=bmask_f[:], in_=ident[:].rearrange("p (b r) -> p b r", r=16), axis=AX.X, op=ALU.add
        )
        nc.vector.tensor_copy(out=bmask[:], in_=bmask_f[:])
        gp_f = keep([128, 4], F32, "gp_f")
        nc.gpsimd.tensor_copy(out=gp_f[:], in_=gp_b[:])
        wpp = keep([128, 2 * O], U8, "wpp")
        wpp_sc = keep([128, O], U8, "wpp_sc")
        for g in range(2):
            nc.gpsimd.tensor_copy(
                out=wpp[:, 1024 * g : 1024 * (g + 1)].rearrange("p (t m c) -> p t m c", t=4, c=2),
                in_=wp_sb[:, 1024 * g : 1024 * (g + 1)].rearrange("p (m t c) -> p t m c", t=4, c=2),
            )
            nc.gpsimd.tensor_copy(
                out=wpp_sc[:, 512 * g : 512 * (g + 1)].rearrange("p (t m) -> p t m", t=4),
                in_=wp_sc[:, 512 * g : 512 * (g + 1)].rearrange("p (m t) -> p t m", t=4),
            )

        egs = {}
        cod = {}
        zb = {}
        ys = {}
        S = {}

        def eg_step(c):
            T, cc = divmod(c, CPT)
            eg = sb([128, 4, BT, 4], BF16, "eg", 3)
            s = 0
            while s < 4:
                m, j = pair_of(4 * cc + s)
                n = 1
                nc.vector.tensor_tensor(
                    out=eg[:, s, :, :].rearrange("p (c i) t -> p c t i", i=4),
                    in0=vg[T][:, m - 1, :, :].rearrange("p t (c i) -> p c t i", i=4),
                    in1=vT[T][:, j, :, :].rearrange("p (c i) t -> p c t i", i=4),
                    op=ALU.mult,
                )
                s += n
            egs[c] = eg

        def q_step(c):
            eg = egs.pop(c)
            codes = sb([128, 512], U32, "codes", 3)
            scales = sb([128, 512], U8, "scales", 3)
            nc.vector.quantize_mx(
                out=codes[:].bitcast(FP8X4),
                scales=scales[:],
                in_=eg[:].rearrange("p s b t -> p (s b t)"),
            )
            cod[c] = (codes, scales)

        def mx_step(c, a):
            codes, scales = cod[c]
            z = ps([128, 512], F32, "z", 4)
            for rep in range(REP[a]):
                nc.tensor.matmul_mx(
                    out=z[:],
                    lhsT=wa_sb[:, 256 * a : 256 * (a + 1)].bitcast(FP4X4),
                    lhsT_scale=wa_sc[:, 128 * a : 128 * (a + 1)],
                    rhs=codes[:].bitcast(FP8X4),
                    rhs_scale=scales[:],
                    start=True,
                    stop=True,
                )
            zb.setdefault(c, {})[a] = z

        def relu_out(z, a):
            y = sb([128, 512], F32, "y", 11)
            nc.scalar.activation(
                out=y[:], in_=z[:], func=ACTF.Relu, bias=bac[:, a : a + 1], scale=1.0
            )
            return y

        def evac_step(c):
            zz = zb[c]
            if MODES[c]:
                parts = []
                for i in range(2):
                    y = relu_out(zz[2 * i], 2 * i)
                    yc = sb([128, 512], F32, "yc", 5)
                    nc.scalar.activation(
                        out=yc[:],
                        in_=y[:],
                        func=ACTF.Identity,
                        scale=ratio[:, i : i + 1],
                        bias=bac[:, 2 * i + 1 : 2 * i + 2],
                    )
                    parts.append(yc)
                ys[c] = parts
            else:
                ys[c] = [(relu_out(zz[a], a), wide[:, a, :]) for a in range(4)]

        def stt_step(c):
            if not MODES[c]:
                return
            parts = []
            for i in range(2):
                r = sb([128, 512], F32, "r", 5)
                nc.vector.scalar_tensor_tensor(
                    out=r[:],
                    in0=zb[c][2 * i + 1][:],
                    scalar=nba[:, 2 * i + 1 : 2 * i + 2],
                    in1=ys[c][i][:],
                    op0=ALU.max,
                    op1=ALU.add,
                )
                parts.append((r, wide[:, 4 + i, :]))
            ys[c] = parts

        def comb_step(c):
            if MODES[c] != 2:
                return
            (r0, w0), (r1, w1) = ys[c]
            r = sb([128, 512], F32, "rr", 3)
            nc.vector.scalar_tensor_tensor(
                out=r[:], in0=r0[:], scalar=ratio2[:], in1=r1[:], op0=ALU.mult, op1=ALU.add
            )
            ys[c] = [(r, w1)]

        def score_step(c, s):
            T, cc = divmod(c, CPT)
            if cc == 0 and s == 0:
                S[T] = ps([128, NP, SW], F32, "s", 1)
            parts = ys[c]
            col = 4 * cc + s
            for i, (y, w) in enumerate(parts):
                nc.tensor.matmul(
                    S[T][:, col, :],
                    lhsT=y[:, 128 * s : 128 * (s + 1)],
                    rhs=w,
                    start=(i == 0),
                    stop=(i == len(parts) - 1),
                )

        st = {}

        def soft_a(T):
            ssb = sb([128, NP], F32, "ssb", 2)
            nc.vector.tensor_copy(out=ssb[:], in_=S.pop(T)[:, :, 0])
            mx = sb([128, 1], F32, "mx", 2)
            nc.vector.tensor_reduce(out=mx[:], in_=ssb[:], axis=AX.X, op=ALU.max)
            nmx = sb([128, 1], F32, "nmx", 2)
            nc.vector.tensor_scalar(
                out=nmx[:], in0=mx[:], scalar1=-1.0, scalar2=None, op0=ALU.mult
            )
            st["soft", T] = (ssb, nmx)

        def soft_exp(T):
            ssb, nmx = st.pop(("soft", T))
            e = sb([128, NP], F32, "e", 2)
            zs = sb([128, 1], F32, "zs", 2)
            nc.scalar.activation(
                out=e[:], in_=ssb[:], func=ACTF.Exp, bias=nmx[:], scale=1.0, accum_out=zs[:]
            )
            st["exp", T] = (e, zs)

        def soft_b(T):
            e, zs = st.pop(("exp", T))
            rz = sb([128, 1], F32, "rz", 2)
            nc.vector.reciprocal(out=rz[:], in_=zs[:])
            al = sb([128, NP], F32, "al", 2)
            nc.vector.tensor_scalar(
                out=al[:], in0=e[:], scalar1=rz[:], scalar2=None, op0=ALU.mult
            )
            cp = comps[T % 2]
            nc.vector.tensor_copy(out=cp[:, 0:NP, 0], in_=al[:])
            nc.vector.tensor_tensor(
                out=cp[:, 0:NP, 1], in0=al[:], in1=cp[:, 0:NP, 0], op=ALU.subtract
            )

        def al_tr(T):
            bank = ps([128, 128], BF16, "m", 3)
            nc.tensor.transpose(
                bank[:], comps[T % 2][:].rearrange("p k c -> p (k c)"), ident_b[:]
            )
            st["alb", T] = bank

        def al_copy(T):
            bank = st.pop(("alb", T))
            alT = sb([128, 128], BF16, "alT", 2)
            nc.scalar.copy(out=alT[:], in_=bank[:])
            st["alT", T] = alT

        def sel(T):
            alT = st.pop(("alT", T))
            bank = ps([128, F - 1, 16], F32, "m", 3)
            rhs = alT[:].rearrange("p (g b) -> p b g", b=8)
            for m in range(F - 1):
                for b in range(8):
                    nc.tensor.matmul(
                        bank[:, m, :],
                        lhsT=wsel[:, m, 112 - 16 * b : 240 - 16 * b],
                        rhs=rhs[:, b, :],
                        start=(b == 0),
                        stop=(b == 7),
                    )
            st["sel", T] = bank

        def make_ap(T):
            bank = st.pop(("sel", T))
            ap = sb([128, 16, F - 1, 8], BF16, "ap", 2)
            nc.vector.tensor_tensor(
                out=ap[:],
                in0=bank[:].rearrange("p m g -> p g m").unsqueeze(3).to_broadcast([128, 16, F - 1, 8]),
                in1=bmask[:].unsqueeze(1).unsqueeze(1).to_broadcast([128, 16, F - 1, 8]),
                op=ALU.mult,
            )
            st["ap", T] = ap

        def pool_mm(T, dg):
            ap = st["ap", T]
            bank = ps([128, 4, F - 1, 16], F32, *(("z", 4) if T == NT - 1 else ("m", 3)))
            for gi in range(2):
                g = 2 * dg + gi
                for t in range(4):
                    nc.tensor.matmul(
                        bank[:, t, :, 8 * gi : 8 * gi + 8],
                        lhsT=vd[T][:, g, t : D : 4],
                        rhs=ap[:, g, :, :],
                        start=True,
                        stop=True,
                    )
            st["pm", T, dg] = bank

        def pool_mul(T, dg):
            bank = st.pop(("pm", T, dg))
            if dg == 0:
                st["q", T] = sb([128, 4, F - 1, BT], F32, "q", 2)
            q = st["q", T]
            nc.vector.tensor_tensor(
                out=q[:, :, :, 16 * dg : 16 * dg + 16],
                in0=bank[:],
                in1=vT[T][:, 1:F, 16 * dg : 16 * dg + 16, :].rearrange("p m b t -> p t m b"),
                op=ALU.mult,
            )

        def pool_sum(T):
            q = st.pop(("q", T))
            bank = ps([128, 4, 128], F32, "m", 3)
            for t in range(4):
                for m in range(F - 1):
                    nc.tensor.matmul(
                        bank[:, t, :],
                        lhsT=q[:, t, m, :],
                        rhs=ident[:],
                        start=(m == 0),
                        stop=(m == F - 2),
                        is_transpose=True,
                    )
            st["sum", T] = bank

        def sum_copy(T):
            bank = st.pop(("sum", T))
            psb = sb([128, 4, 128], F32, "psb", 2)
            nc.scalar.copy(out=psb[:], in_=bank[:])
            st["psb", T] = psb

        def pool_back(T):
            psb = st.pop(("psb", T))
            bank = ps([128, 4, BT], F32, "m", 3)
            for t in range(4):
                nc.tensor.transpose(bank[:, t, :], psb[:, t, :], ident[:])
            st["back", T] = bank

        def pool_gain(T):
            bank = st.pop(("back", T))
            pl = sb([128, BT, 4], BF16, "pl", 2)
            nc.vector.tensor_tensor(
                out=pl[:],
                in0=bank[:].rearrange("p t b -> p b t"),
                in1=gp_f[:].unsqueeze(1).to_broadcast([128, BT, 4]),
                op=ALU.mult,
            )
            st["pl", T] = pl

        osc = keep([128, 2, B], U8, "osc")

        def head_q(T):
            pl = st.pop(("pl", T))
            pc = sb([128, BT], U32, "pc", 2)
            psc = sb([128, BT], U8, "psc", 2)
            nc.vector.quantize_mx(
                out=pc[:].bitcast(FP8X4), scales=psc[:], in_=pl[:].rearrange("p b t -> p (b t)")
            )
            st["pc", T] = (pc, psc)

        def head_p(T, g):
            pc, psc = st["pc", T]
            bank = ps([128, 4, BT], F32, "m", 3)
            for t in range(4):
                col = 512 * g + 128 * t
                nc.tensor.matmul_mx(
                    out=bank[:, t, :],
                    lhsT=wpp[:, 2 * col : 2 * col + 256].bitcast(FP4X4),
                    lhsT_scale=wpp_sc[:, col : col + 128],
                    rhs=pc[:].bitcast(FP8X4),
                    rhs_scale=psc[:],
                    start=True,
                    stop=True,
                )
            st["pbank", T, g] = bank

        def head_pe(T, g):
            bank = st.pop(("pbank", T, g))
            pb = sb([128, BT, 4], BF16, "pb", 4)
            nc.scalar.copy(out=pb[:], in_=bank[:].rearrange("p t b -> p b t"))
            st["pb", T, g] = pb

        def head_pq(T, g):
            pb = st.pop(("pb", T, g))
            oc = sb([128, BT], U32, "oc", 4)
            nc.vector.quantize_mx(
                out=oc[:].bitcast(FP8X4),
                scales=osc[:, g, BT * T : BT * (T + 1)],
                in_=pb[:].rearrange("p b t -> p (b t)"),
            )
            nc.sync.dma_start(
                out=out_words[g, :, BT * T : BT * (T + 1), :]
                .rearrange("p m t -> p (m t)")
                .bitcast(I32),
                in_=oc[:].bitcast(I32),
            )
            if T == NT - 1:
                for q in range(4):
                    eng = nc.sync if q % 2 else nc.scalar
                    eng.dma_start(
                        out=out_scales[g, 4 * q : 4 * q + 4, :].bitcast(I32),
                        in_=osc[32 * q : 32 * q + 4, g, :].bitcast(I32),
                    )

        def head_o(T, hf):
            pc, psc = st["pc", T]
            bank = ps([128, 512], F32, "m", 3)
            nc.tensor.matmul_mx(
                out=bank[:],
                lhsT=pc[:].bitcast(FP8X4),
                lhsT_scale=psc[:],
                rhs=wp_sb[:, 1024 * hf : 1024 * (hf + 1)].bitcast(FP4X4),
                rhs_scale=wp_sc[:, 512 * hf : 512 * (hf + 1)],
                start=True,
                stop=True,
            )
            st["obank", T, hf] = bank

        def head_oe(T, hf):
            bank = st.pop(("obank", T, hf))
            o = sb([128, 512], F32, "o", 4)
            nc.scalar.copy(out=o[:], in_=bank[:])
            nc.sync.dma_start(
                out=out[BT * T : BT * (T + 1), 512 * hf : 512 * (hf + 1)], in_=o[:]
            )

        pre = {
            3: [(al_copy,)],
            4: [(make_ap,)],
            5: [(pool_mul, 0), (pool_mul, 1)],
            6: [(pool_mul, 2), (pool_mul, 3)],
            7: [(pool_mul, 4), (pool_mul, 5)],
            8: [(pool_mul, 6), (pool_mul, 7)],
            9: [(sum_copy,)],
            10: [(pool_gain,)],
            11: [(head_pe, 0), (head_oe, 0)],
            12: [(head_pe, 1), (head_pq, 0)],
            13: [(head_oe, 1), (head_pq, 1)],
        }
        mid = {2: [(soft_b,)], 10: [(head_q,)]}
        pes = {
            2: [(al_tr,)],
            3: [(sel,)],
            4: [(pool_mm, 0), (pool_mm, 1)],
            5: [(pool_mm, 2), (pool_mm, 3)],
            6: [(pool_mm, 4), (pool_mm, 5)],
            7: [(pool_mm, 6), (pool_mm, 7)],
            8: [(pool_sum,)],
            9: [(pool_back,)],
            10: [(head_p, 0), (head_o, 0)],
            11: [(head_p, 1)],
            12: [(head_o, 1)],
        }
        prep_at = {}
        for T in range(1, NT):
            for q, k in ((0, 0), (2, 1), (3, 2), (5, 3)):
                prep_at.setdefault(CPT * (T - 1) + q + (1 if T == 1 and q < 1 else 0), []).append((T, k))
        late = []
        eg_step(0)

        for n in range(NCH + 14):
            offs = [(T, n - CPT * (T + 1)) for T in range(NT) if 0 <= n - CPT * (T + 1) <= 13]
            offs.reverse()

            def run(table):
                for T, o in offs:
                    for f, *args in table.get(o, []):
                        f(T, *args)

            for T, o in offs:
                if o == 2:
                    soft_a(T)
            if n < NCH:
                q_step(n)
                mx_step(n, 0)
                mx_step(n, 2)
            if 2 <= n <= NCH + 1:
                score_step(n - 2, 0)
                score_step(n - 2, 1)
            if 1 <= n <= NCH:
                stt_step(n - 1)
            if n < NCH:
                mx_step(n, 1)
            if 2 <= n <= NCH + 1:
                score_step(n - 2, 2)
                score_step(n - 2, 3)
            if n < NCH:
                mx_step(n, 3)
            for T, o in offs:
                if o == 2:
                    soft_exp(T)
            run(pre)
            if n < NCH:
                evac_step(n)
            for T, k in late:
                prep_act(T, k)
            late = []
            if n + 1 < NCH:
                eg_step(n + 1)
            if 1 <= n <= NCH:
                comb_step(n - 1)
            run(mid)
            run(pes)
            for T, k in prep_at.get(n, []):
                prep_tr(T, k)
                late.append((T, k))
            if n % CPT == 0 and n // CPT + 2 < NT:
                load_vb(n // CPT + 2)
            if n % CPT == 0 and 0 < n // CPT < NT:
                load_vd(n // CPT)
